import numpy as np
import ml_dtypes


def mxq(x, axis, fmt="e4m3"):
    dtype, down = {"e4m3": (ml_dtypes.float8_e4m3fn, 7), "e5m2": (ml_dtypes.float8_e5m2, 14)}[fmt]
    v = np.moveaxis(np.asarray(x, np.float32).astype(ml_dtypes.bfloat16).astype(np.float64), axis, -1)
    blocks = v.reshape(v.shape[:-1] + (-1, 32))
    amax = np.abs(blocks).max(-1, keepdims=True)
    byte = np.maximum(np.where(amax > 0, np.frexp(amax)[1] - 1 + 127, 0) - down, 1)
    scale = np.exp2(byte - 127.0)
    codes = (blocks / scale).astype(np.float32).astype(dtype).astype(np.float64)
    return np.moveaxis((codes * scale).reshape(v.shape), -1, axis)


WIDE = False


def mx_kscale(k):
    if not WIDE:
        return np.ones(k)
    levels = np.array([10, -10, 5, -5, 0])
    if k % 512:
        return np.exp2(np.random.permutation(np.resize(levels, k // 32))).repeat(32)
    a = np.empty((k // 512, 16))
    for p in range(k // 512):
        a[p, :8] = np.random.permutation(np.resize(levels, 8))
        for g in range(8):
            far = levels[np.abs(levels - a[p, g]) >= 10]
            a[p, g + 8] = far[np.random.randint(len(far))]
    return np.exp2(a.ravel()).repeat(32)


def f64(x):
    return np.asarray(x).astype(np.float64)


def striped(idx):
    return np.tile(idx.reshape(-1, 16).T, (8, 1)).astype(np.uint16)


def unstriped(offs):
    return offs[:16].T.reshape(-1).astype(np.int64)


def striped8(idx):
    return np.concatenate([x.reshape(-1, 16).T for x in idx]).astype(np.uint16)


def runs(offs, k):
    lists = np.stack([offs[16 * r : 16 * r + 16].T.reshape(-1) for r in range(8)]).astype(np.int64)
    return lists[np.arange(k) % 512 // 64]


def pack_weight(w):
    k, n = w.shape
    w = f64(np.asarray(w, np.float32).astype(ml_dtypes.bfloat16)).reshape(k // 32, 32, n)
    amax = np.abs(w).max(1)
    byte = np.clip(np.where(amax > 0, np.frexp(amax)[1] - 1 + 127 - 7, 1), 1, 254)
    scaled = (w * np.exp2(127.0 - byte)[:, None, :]).reshape(k, n).astype(np.float32)
    words = np.ascontiguousarray(scaled.reshape(k // 512, 128, 4, n).transpose(0, 1, 3, 2)).astype(ml_dtypes.float8_e4m3fn).view(np.uint8)
    return words, np.ascontiguousarray(byte.astype(np.uint8).reshape(k // 512, 16, n))


def unpack_weight(words, scales):
    g, p, n, _ = words.shape
    vals = np.ascontiguousarray(words).view(ml_dtypes.float8_e4m3fn).astype(np.float64) * np.repeat(np.exp2(scales.astype(np.float64) - 127.0), 8, axis=1)[..., None]
    return vals.transpose(0, 1, 3, 2).reshape(g * 512, n)


def sigmoid(v):
    return 1.0 / (1.0 + np.exp(-np.maximum(v, -700.0)))

def planes(y):
    n, m = y.shape
    v = y.astype(np.float32).astype(ml_dtypes.bfloat16).astype(np.float64).reshape(n // 32, 32, m)
    top = np.abs(v).max(1)
    byte = np.clip(np.where(top > 0, np.frexp(top)[1] - 1 + 127 - 7, 1), 1, 254)
    codes = (v * np.exp2(127.0 - byte)[:, None, :]).reshape(n, m).astype(np.float32).astype(ml_dtypes.float8_e4m3fn).view(np.uint8)
    words = codes.reshape(n // 512, 128, 4, m).transpose(0, 1, 3, 2)
    return np.ascontiguousarray(words), np.ascontiguousarray(byte.astype(np.uint8).reshape(n // 512, 16, m))


K, T, S, N, H, W = 512, 2048, 512, 512, 512, 2048


def setup_inputs():
    n = np.random.standard_normal
    s = mx_kscale(K)[:, None]
    u = mx_kscale(H)
    packed_xT = pack_weight(n((K, T)) * s)
    packed_w1 = pack_weight(n((K, H)) / np.sqrt(K) / s)
    packed_w2 = pack_weight(n((H, N)) / np.sqrt(H) / u[:, None])
    return {
        "x_words": packed_xT[0],
        "x_scales": packed_xT[1],
        "w1_words": packed_w1[0],
        "w1_scales": packed_w1[1],
        "tau": np.random.uniform(0.5, 1.2, (H, 1)).astype(np.float32),
        "gn": (np.random.uniform(0.5, 1.5, (H, 1)) * u[:, None]).astype(np.float32),
        "w2_words": packed_w2[0],
        "w2_scales": packed_w2[1],
        "sl": np.random.uniform(1.5, 3.0, (N, 1)).astype(np.float32),
        "th": (0.5 * n((N, 1))).astype(np.float32),
        "offs": striped(np.random.permutation(T)[:S]),
        "n1": striped8(np.stack([np.random.permutation(S) for _ in range(8)])),
        "n2": striped8(np.stack([np.random.permutation(S) for _ in range(8)])),
        "n3": striped(np.random.randint(0, S, W)),
    }


def reference(x_words, x_scales, w1_words, w1_scales, tau, gn, w2_words, w2_scales, sl, th, offs, n1, n2, n3):
    xq = unpack_weight(x_words, x_scales)[:, unstriped(offs)]
    y = unpack_weight(w1_words, w1_scales).T @ xq
    sz = np.abs(y)
    ea = np.exp(-1.0 * (f64(tau) * (sz[np.arange(H)[:, None], runs(n1, H)])))
    z = f64(gn) * ((y - (y[np.arange(H)[:, None], runs(n2, H)])) * ea)
    h = unpack_weight(w2_words, w2_scales).T @ mxq(z, 0, "e4m3")
    sg = sigmoid(f64(sl) * (h[:, unstriped(n3)] - f64(th)))
    cnt = sg.reshape(N, S, 4).sum(axis=2)
    out_0 = np.maximum(h, cnt + -1.5)
    return (out_0,) + planes(out_0)

@@ -1,0 +1,217 @@
+from contextlib import ExitStack
+
+import concourse.mybir as mybir
+
+F32 = mybir.dt.float32
+BF16 = mybir.dt.bfloat16
+I32 = mybir.dt.int32
+U32 = mybir.dt.uint32
+U16 = mybir.dt.uint16
+U8 = mybir.dt.uint8
+FP8X4 = mybir.dt.float8_e4m3fn_x4
+ALU = mybir.AluOpType
+ACT = mybir.ActivationFunctionType
+AX = mybir.AxisListType
+
+P = 128
+PACK = 4
+T = 2048
+S = 512
+MEMBERS = 4
+CHUNKS = ((0, 256), (256, 384), (384, 512))
+W1_ROW = 4
+W2_ROW = 8
+Y_WINDOW = 1024
+H_WINDOW = 2048
+
+FLOPS = 2 * 2 * 512 * 512 * 512
+
+
+def tile_picked_layelaegc_none_po_kernel(
+    tc, x_words, x_scales, w1_words, w1_scales, tau, gn, w2_words, w2_scales, sl, th,
+    offs, n1, n2, n3, out_0, out_1, out_2,
+):
+    nc = tc.nc
+
+    def words(ap):
+        return ap[0].rearrange("p c r -> p (c r)").bitcast(I32)
+
+    def per_row(ap):
+        return ap.rearrange("(p t) o -> p (t o)", t=PACK)
+
+    def load_scale_rows(queue, plane, first_row, scales, q):
+        queue.dma_start(
+            out=plane[32 * q + first_row : 32 * q + first_row + 4, :].bitcast(I32),
+            in_=scales[0, 4 * q : 4 * q + 4, :].bitcast(I32),
+        )
+
+    def dealt(tile):
+        return tile[:].rearrange("p (t m) -> p m t", t=PACK)
+
+    def as_loaded(tile):
+        return tile[:].rearrange("p (m t) -> p m t", t=PACK)
+
+    def planes_walk(tile, c0, c1):
+        return tile[:, :, c0:c1].rearrange("p t (c i) -> p c t i", i=4)
+
+    def packed_walk(tile, c0, c1):
+        return tile[:, PACK * c0 : PACK * c1].rearrange("p (c i t) -> p c t i", i=4, t=PACK)
+
+    with ExitStack() as ctx:
+        held = ctx.enter_context(tc.tile_pool(name="held", bufs=1))
+        ring = ctx.enter_context(tc.tile_pool(name="ring", bufs=3))
+        psum = ctx.enter_context(tc.psum_pool(name="psum", bufs=1))
+
+        offs_t = held.tile([P, S // 16], U16, name="offs_t")
+        n1_t = held.tile([P, S // 16], U16, name="n1_t")
+        n2_t = held.tile([P, S // 16], U16, name="n2_t")
+        n3_t = held.tile([P, MEMBERS * S // 16], U16, name="n3_t")
+        xw = held.tile([P, T], U32, name="xw", align_bytes=64)
+        xs = held.tile([P, T], U8, name="xs", align_bytes=64)
+        w1w_in = held.tile([P, S], I32, name="w1w_in", align_bytes=64)
+        w2w_in = held.tile([P, S], U32, name="w2w_in", align_bytes=64)
+        w1s_in = held.tile([P, S], U8, name="w1s_in", align_bytes=64)
+        w2s_in = held.tile([P, S], U8, name="w2s_in", align_bytes=64)
+        w1w = held.tile([P, S], I32, name="w1w", align_bytes=64)
+        w2w = held.tile([P, S], U32, name="w2w", align_bytes=64)
+        w1s = held.tile([P, S], U8, name="w1s", align_bytes=64)
+        w2s = held.tile([P, S], U8, name="w2s", align_bytes=64)
+        gn_t = held.tile([P, PACK], F32, name="gn_t")
+        tau_t = held.tile([P, PACK], F32, name="tau_t")
+        sl_t = held.tile([P, PACK], F32, name="sl_t")
+        th_t = held.tile([P, PACK], F32, name="th_t")
+        neg_tau = held.tile([P, PACK], F32, name="neg_tau")
+        sl_th = held.tile([P, PACK], F32, name="sl_th")
+        neg_sl_th = held.tile([P, PACK], F32, name="neg_sl_th")
+
+        nc.vector.memset(xs[:].bitcast(I32), 0)
+        nc.vector.memset(w1s_in[:].bitcast(I32), 0)
+        nc.gpsimd.memset(w2s_in[:].bitcast(I32), 0)
+
+        nc.sync.dma_start(offs_t[:], offs)
+        nc.sync.dma_start(out=w1w_in[:], in_=words(w1_words))
+        for q in range(4):
+            load_scale_rows(nc.sync, xs, 0, x_scales, q)
+        nc.sync.dma_start(out=xw[:].bitcast(I32), in_=words(x_words))
+        for q in range(4):
+            load_scale_rows(nc.sync, w1s_in, W1_ROW, w1_scales, q)
+        nc.sync.dma_start(n2_t[:], n2)
+        nc.sync.dma_start(out=w2w_in[:].bitcast(I32), in_=words(w2_words))
+        nc.sync.dma_start(n1_t[:], n1)
+        nc.sync.dma_start(n3_t[:], n3)
+        for q in range(4):
+            load_scale_rows(nc.sync, w2s_in, W2_ROW, w2_scales, q)
+        nc.gpsimd.dma_start(out=gn_t[:], in_=per_row(gn))
+        nc.gpsimd.dma_start(out=tau_t[:], in_=per_row(tau))
+        nc.gpsimd.dma_start(out=sl_t[:], in_=per_row(sl))
+        nc.gpsimd.dma_start(out=th_t[:], in_=per_row(th))
+
+        nc.scalar.activation(neg_tau[:], tau_t[:], ACT.Copy, scale=-1.0)
+        nc.scalar.copy(dealt(w2w), as_loaded(w2w_in))
+
+        gw = held.tile([P, S], U32, name="gw", align_bytes=64)
+        gs = held.tile([P, S], U8, name="gs", align_bytes=64)
+        nc.vector.tensor_copy(dealt(w1w), as_loaded(w1w_in))
+        nc.vector.tensor_copy(gs[:], xs[:].indirect(offs_t[:]))
+        nc.vector.tensor_copy(gw[:], xw[:].indirect(offs_t[:]))
+        for t in range(PACK):
+            nc.vector.tensor_copy(w1s[:, P * t : P * (t + 1)], w1s_in[:, t::PACK])
+
+        nc.gpsimd.tensor_tensor(sl_th[:], sl_t[:], th_t[:], ALU.mult)
+        nc.gpsimd.tensor_scalar(neg_sl_th[:], sl_th[:], -1.0, 0.0, ALU.mult, ALU.add)
+        nc.gpsimd.tensor_copy(dealt(w2s), as_loaded(w2s_in))
+
+        y_ps = [psum.tile([P, S], F32, name="y_ps%d" % t) for t in range(PACK)]
+        for t in range(PACK):
+            cols = slice(P * t, P * (t + 1))
+            nc.tensor.matmul_mx(
+                out=y_ps[t][:], lhsT=w1w[:, cols].bitcast(FP8X4), lhsT_scale=w1s[W1_ROW:P, cols],
+                rhs=gw[:].bitcast(FP8X4), rhs_scale=gs[:], start=True, stop=True,
+            )
+
+        yg = [held.tile([P, Y_WINDOW], F32, name="yg%d" % t) for t in range(PACK)]
+        sz = [held.tile([P, S], F32, name="sz%d" % t) for t in range(PACK)]
+        fetched = held.tile([P, PACK, S], F32, name="fetched")
+        diff = held.tile([P, PACK, S], F32, name="diff")
+        ea = held.tile([P, PACK, S], F32, name="ea")
+
+        nc.vector.tensor_scalar(yg[0][:, :S], y_ps[0][:], gn_t[:, 0:1], None, ALU.mult)
+        for t in range(PACK):
+            if t + 1 < PACK:
+                nc.scalar.activation(yg[t + 1][:, :S], y_ps[t + 1][:], ACT.Copy, scale=gn_t[:, t + 1 : t + 2])
+            nc.scalar.activation(sz[t][:], y_ps[t][:], ACT.Abs)
+        for t in range(PACK):
+            nc.vector.tensor_copy(fetched[:, t, :], yg[t][:].indirect(n2_t[:]))
+            nc.vector.tensor_tensor(diff[:, t, :], yg[t][:, :S], fetched[:, t, :], ALU.subtract)
+
+        zb = held.tile([P, PACK * S], BF16, name="zb", align_bytes=64)
+        zw = held.tile([P, S], U32, name="zw", align_bytes=64)
+        zs = held.tile([P, S], U8, name="zs", align_bytes=64)
+        h_ps = [psum.tile([P, S], F32, name="h_ps%d" % t) for t in range(PACK)]
+        h = [held.tile([P, H_WINDOW], F32, name="h%d" % t) for t in range(PACK)]
+        last0 = CHUNKS[-1][0]
+        h0_last = psum.tile([P, S], F32, name="y_ps0")
+
+        for c0, c1 in CHUNKS:
+            for t in range(PACK):
+                nc.scalar.activation(
+                    ea[:, t, c0:c1], sz[t][:].indirect(n1_t[:, c0 // 16 : c1 // 16]), ACT.Exp,
+                    scale=neg_tau[:, t : t + 1],
+                )
+            nc.vector.tensor_tensor(
+                packed_walk(zb, c0, c1), planes_walk(diff, c0, c1), planes_walk(ea, c0, c1), ALU.mult
+            )
+            nc.vector.quantize_mx(
+                out=zw[:, c0:c1].bitcast(FP8X4), scales=zs[:, c0:c1], in_=zb[:, PACK * c0 : PACK * c1]
+            )
+            for t in range(PACK):
+                cols = slice(P * t, P * (t + 1))
+                bank = h0_last if (t == 0 and c0 == last0) else h_ps[t]
+                nc.tensor.matmul_mx(
+                    out=bank[:, c0:c1], lhsT=w2w[:, cols].bitcast(FP8X4), lhsT_scale=w2s[W2_ROW:P, cols],
+                    rhs=zw[:, c0:c1].bitcast(FP8X4), rhs_scale=zs[:, c0:c1], start=True, stop=True,
+                )
+            if c1 == last0:
+                nc.vector.tensor_copy(h[0][:, :last0], h_ps[0][:, :last0])
+        nc.vector.tensor_copy(h[0][:, last0:S], h0_last[:, last0:S])
+        for t in range(1, PACK):
+            nc.vector.tensor_copy(h[t][:, :S], h_ps[t][:])
+
+        res = held.tile([P, PACK, S], F32, name="res")
+        rb = held.tile([P, PACK * S], BF16, name="rb", align_bytes=64)
+        rw = held.tile([P, S], U32, name="rw", align_bytes=64)
+        rs = held.tile([P, S], U8, name="rs", align_bytes=64)
+        out_rows = out_0.rearrange("(p t) c -> p t c", t=PACK)
+        out_words = words(out_1)
+
+        for c0, c1 in CHUNKS:
+            n = c1 - c0
+            for t in range(PACK):
+                sg = ring.tile([P, MEMBERS * CHUNKS[0][1]], F32, name="sg")
+                cnt = ring.tile([P, CHUNKS[0][1]], F32, name="cnt")
+                nc.scalar.activation(
+                    sg[:, : MEMBERS * n],
+                    h[t][:].indirect(n3_t[:, MEMBERS * c0 // 16 : MEMBERS * c1 // 16]),
+                    ACT.Sigmoid, bias=neg_sl_th[:, t : t + 1], scale=sl_t[:, t : t + 1],
+                )
+                nc.vector.tensor_reduce(
+                    cnt[:, :n], sg[:, : MEMBERS * n].rearrange("p (j m) -> p j m", m=MEMBERS), AX.X, ALU.add
+                )
+                nc.vector.scalar_tensor_tensor(
+                    res[:, t, c0:c1], cnt[:, :n], -1.5, h[t][:, c0:c1], ALU.add, ALU.max
+                )
+                if c0 == last0:
+                    nc.sync.dma_start(out=out_rows[:, t, c0:c1], in_=res[:, t, c0:c1])
+            if c0 != last0:
+                nc.sync.dma_start(out=out_rows[:, :, c0:c1], in_=res[:, :, c0:c1])
+            nc.vector.tensor_copy(packed_walk(rb, c0, c1), planes_walk(res, c0, c1))
+            nc.vector.quantize_mx(
+                out=rw[:, c0:c1].bitcast(FP8X4), scales=rs[:, c0:c1], in_=rb[:, PACK * c0 : PACK * c1]
+            )
+            nc.sync.dma_start(out=out_words[:, c0:c1], in_=rw[:, c0:c1].bitcast(I32))
+        for q in range(4):
+            queue = nc.sync if q == 0 else nc.scalar
+            queue.dma_start(
+                out=out_2[0, 4 * q : 4 * q + 4, :].bitcast(I32),
+                in_=rs[32 * q : 32 * q + 4, :].bitcast(I32),
+            )

@@ -46,10 +46,10 @@ def tile_picked_layelaegc_none_po_kernel(
         )
 
     def dealt(tile):
-        return tile[:].rearrange("p (t m) -> p m t", t=PACK)
+        return tile[:].rearrange("p (t m) -> p t m", t=PACK)
 
     def as_loaded(tile):
-        return tile[:].rearrange("p (m t) -> p m t", t=PACK)
+        return tile[:].rearrange("p (m t) -> p t m", t=PACK)
 
     def planes_walk(tile, c0, c1):
         return tile[:, :, c0:c1].rearrange("p t (c i) -> p c t i", i=4)
@@ -68,11 +68,11 @@ def tile_picked_layelaegc_none_po_kernel(
         n3_t = held.tile([P, MEMBERS * S // 16], U16, name="n3_t")
         xw = held.tile([P, T], U32, name="xw", align_bytes=64)
         xs = held.tile([P, T], U8, name="xs", align_bytes=64)
-        w1w_in = held.tile([P, S], I32, name="w1w_in", align_bytes=64)
+        w1w_in = held.tile([P, S], U32, name="w1w_in", align_bytes=64)
         w2w_in = held.tile([P, S], U32, name="w2w_in", align_bytes=64)
         w1s_in = held.tile([P, S], U8, name="w1s_in", align_bytes=64)
         w2s_in = held.tile([P, S], U8, name="w2s_in", align_bytes=64)
-        w1w = held.tile([P, S], I32, name="w1w", align_bytes=64)
+        w1w = held.tile([P, S], U32, name="w1w", align_bytes=64)
         w2w = held.tile([P, S], U32, name="w2w", align_bytes=64)
         w1s = held.tile([P, S], U8, name="w1s", align_bytes=64)
         w2s = held.tile([P, S], U8, name="w2s", align_bytes=64)
@@ -89,15 +89,16 @@ def tile_picked_layelaegc_none_po_kernel(
         nc.gpsimd.memset(w2s_in[:].bitcast(I32), 0)
 
         nc.sync.dma_start(offs_t[:], offs)
-        nc.sync.dma_start(out=w1w_in[:], in_=words(w1_words))
+        nc.sync.dma_start(out=xw[:, : T // 2].bitcast(I32), in_=words(x_words)[:, : T // 2])
         for q in range(4):
             load_scale_rows(nc.sync, xs, 0, x_scales, q)
-        nc.sync.dma_start(out=xw[:].bitcast(I32), in_=words(x_words))
+        nc.sync.dma_start(out=xw[:, T // 2 :].bitcast(I32), in_=words(x_words)[:, T // 2 :])
         for q in range(4):
             load_scale_rows(nc.sync, w1s_in, W1_ROW, w1_scales, q)
+        nc.sync.dma_start(out=w1w_in[:].bitcast(I32), in_=words(w1_words))
         nc.sync.dma_start(n2_t[:], n2)
-        nc.sync.dma_start(out=w2w_in[:].bitcast(I32), in_=words(w2_words))
         nc.sync.dma_start(n1_t[:], n1)
+        nc.sync.dma_start(out=w2w_in[:].bitcast(I32), in_=words(w2_words))
         nc.sync.dma_start(n3_t[:], n3)
         for q in range(4):
             load_scale_rows(nc.sync, w2s_in, W2_ROW, w2_scales, q)
@@ -107,11 +108,11 @@ def tile_picked_layelaegc_none_po_kernel(
         nc.gpsimd.dma_start(out=th_t[:], in_=per_row(th))
 
         nc.scalar.activation(neg_tau[:], tau_t[:], ACT.Copy, scale=-1.0)
-        nc.scalar.copy(dealt(w2w), as_loaded(w2w_in))
+        for t in range(PACK):
+            nc.scalar.copy(w1w[:, P * t : P * (t + 1)], w1w_in[:, t::PACK])
 
         gw = held.tile([P, S], U32, name="gw", align_bytes=64)
         gs = held.tile([P, S], U8, name="gs", align_bytes=64)
-        nc.vector.tensor_copy(dealt(w1w), as_loaded(w1w_in))
         nc.vector.tensor_copy(gs[:], xs[:].indirect(offs_t[:]))
         nc.vector.tensor_copy(gw[:], xw[:].indirect(offs_t[:]))
         for t in range(PACK):
@@ -119,15 +120,22 @@ def tile_picked_layelaegc_none_po_kernel(
 
         nc.gpsimd.tensor_tensor(sl_th[:], sl_t[:], th_t[:], ALU.mult)
         nc.gpsimd.tensor_scalar(neg_sl_th[:], sl_th[:], -1.0, 0.0, ALU.mult, ALU.add)
+        nc.gpsimd.tensor_copy(dealt(w2w), as_loaded(w2w_in))
         nc.gpsimd.tensor_copy(dealt(w2s), as_loaded(w2s_in))
 
-        y_ps = [psum.tile([P, S], F32, name="y_ps%d" % t) for t in range(PACK)]
+        half = S // 2
+        y0_low = psum.tile([P, S], F32, name="bank_a")
+        y0_high = psum.tile([P, S], F32, name="bank_b")
+        y_parts = [[(y0_low, 0, half), (y0_high, half, S)]]
+        for t in range(1, PACK):
+            y_parts.append([(psum.tile([P, S], F32, name="y_ps%d" % t), 0, S)])
         for t in range(PACK):
             cols = slice(P * t, P * (t + 1))
-            nc.tensor.matmul_mx(
-                out=y_ps[t][:], lhsT=w1w[:, cols].bitcast(FP8X4), lhsT_scale=w1s[W1_ROW:P, cols],
-                rhs=gw[:].bitcast(FP8X4), rhs_scale=gs[:], start=True, stop=True,
-            )
+            for bank, c0, c1 in y_parts[t]:
+                nc.tensor.matmul_mx(
+                    out=bank[:, c0:c1], lhsT=w1w[:, cols].bitcast(FP8X4), lhsT_scale=w1s[W1_ROW:P, cols],
+                    rhs=gw[:, c0:c1].bitcast(FP8X4), rhs_scale=gs[:, c0:c1], start=True, stop=True,
+                )
 
         yg = [held.tile([P, Y_WINDOW], F32, name="yg%d" % t) for t in range(PACK)]
         sz = [held.tile([P, S], F32, name="sz%d" % t) for t in range(PACK)]
@@ -135,32 +143,51 @@ def tile_picked_layelaegc_none_po_kernel(
         diff = held.tile([P, PACK, S], F32, name="diff")
         ea = held.tile([P, PACK, S], F32, name="ea")
 
-        nc.vector.tensor_scalar(yg[0][:, :S], y_ps[0][:], gn_t[:, 0:1], None, ALU.mult)
+        nc.vector.tensor_scalar(yg[0][:, :half], y0_low[:, :half], gn_t[:, 0:1], None, ALU.mult)
+        nc.scalar.activation(yg[0][:, half:S], y0_high[:, half:S], ACT.Copy, scale=gn_t[:, 0:1])
         for t in range(PACK):
             if t + 1 < PACK:
-                nc.scalar.activation(yg[t + 1][:, :S], y_ps[t + 1][:], ACT.Copy, scale=gn_t[:, t + 1 : t + 2])
-            nc.scalar.activation(sz[t][:], y_ps[t][:], ACT.Abs)
-        for t in range(PACK):
+                nc.scalar.activation(
+                    yg[t + 1][:, :S], y_parts[t + 1][0][0][:], ACT.Copy, scale=gn_t[:, t + 1 : t + 2]
+                )
+            for bank, c0, c1 in y_parts[t]:
+                nc.scalar.activation(sz[t][:, c0:c1], bank[:, c0:c1], ACT.Abs)
+
+        def subtract(t, c0, c1):
+            nc.vector.tensor_tensor(diff[:, t, c0:c1], yg[t][:, c0:c1], fetched[:, t, c0:c1], ALU.subtract)
+
+        last = PACK - 1
+        for t in range(last):
             nc.vector.tensor_copy(fetched[:, t, :], yg[t][:].indirect(n2_t[:]))
-            nc.vector.tensor_tensor(diff[:, t, :], yg[t][:, :S], fetched[:, t, :], ALU.subtract)
+            if t > 0:
+                subtract(t - 1, 0, S)
+        nc.vector.tensor_copy(fetched[:, last, :half], yg[last][:].indirect(n2_t[:, : half // 16]))
+        subtract(last - 1, 0, S)
+        subtract(last, 0, half)
 
         zb = held.tile([P, PACK * S], BF16, name="zb", align_bytes=64)
         zw = held.tile([P, S], U32, name="zw", align_bytes=64)
         zs = held.tile([P, S], U8, name="zs", align_bytes=64)
-        h_ps = [psum.tile([P, S], F32, name="h_ps%d" % t) for t in range(PACK)]
+        h_ps = [psum.tile([P, S], F32, name="h_ps%d" % t) for t in range(PACK - 1)]
+        h_ps.append(psum.tile([P, S], F32, name="bank_b"))
         h = [held.tile([P, H_WINDOW], F32, name="h%d" % t) for t in range(PACK)]
         last0 = CHUNKS[-1][0]
-        h0_last = psum.tile([P, S], F32, name="y_ps0")
+        h0_last = psum.tile([P, S], F32, name="bank_a")
 
-        for c0, c1 in CHUNKS:
+        def decay(c0, c1):
             for t in range(PACK):
                 nc.scalar.activation(
                     ea[:, t, c0:c1], sz[t][:].indirect(n1_t[:, c0 // 16 : c1 // 16]), ACT.Exp,
                     scale=neg_tau[:, t : t + 1],
                 )
+
+        def weigh(c0, c1, t0, t1):
             nc.vector.tensor_tensor(
-                packed_walk(zb, c0, c1), planes_walk(diff, c0, c1), planes_walk(ea, c0, c1), ALU.mult
+                packed_walk(zb, c0, c1)[:, :, t0:t1, :], planes_walk(diff, c0, c1)[:, :, t0:t1, :],
+                planes_walk(ea, c0, c1)[:, :, t0:t1, :], ALU.mult,
             )
+
+        def second_product(c0, c1):
             nc.vector.quantize_mx(
                 out=zw[:, c0:c1].bitcast(FP8X4), scales=zs[:, c0:c1], in_=zb[:, PACK * c0 : PACK * c1]
             )
@@ -171,8 +198,19 @@ def tile_picked_layelaegc_none_po_kernel(
                     out=bank[:, c0:c1], lhsT=w2w[:, cols].bitcast(FP8X4), lhsT_scale=w2s[W2_ROW:P, cols],
                     rhs=zw[:, c0:c1].bitcast(FP8X4), rhs_scale=zs[:, c0:c1], start=True, stop=True,
                 )
-            if c1 == last0:
-                nc.vector.tensor_copy(h[0][:, :last0], h_ps[0][:, :last0])
+
+        for k, (c0, c1) in enumerate(CHUNKS):
+            decay(c0, c1)
+            weigh(c0, c1, 0, PACK // 2 if c0 == last0 else PACK)
+            if k == 0:
+                nc.scalar.activation(fetched[:, last, half:], yg[last][:].indirect(n2_t[:, half // 16 :]), ACT.Copy)
+                subtract(last, half, S)
+            else:
+                b0, b1 = CHUNKS[k - 1]
+                nc.vector.tensor_copy(h[0][:, b0:b1], h_ps[0][:, b0:b1])
+            if c0 == last0:
+                weigh(c0, c1, PACK // 2, PACK)
+            second_product(c0, c1)
         nc.vector.tensor_copy(h[0][:, last0:S], h0_last[:, last0:S])
         for t in range(1, PACK):
             nc.vector.tensor_copy(h[t][:, :S], h_ps[t][:])
@@ -201,16 +239,21 @@ def tile_picked_layelaegc_none_po_kernel(
                     res[:, t, c0:c1], cnt[:, :n], -1.5, h[t][:, c0:c1], ALU.add, ALU.max
                 )
                 if c0 == last0:
-                    nc.sync.dma_start(out=out_rows[:, t, c0:c1], in_=res[:, t, c0:c1])
+                    queue = nc.scalar if t == PACK - 1 else nc.sync
+                    queue.dma_start(out=out_rows[:, t, c0:c1], in_=res[:, t, c0:c1])
+                if c0 == last0 and t % 2 == 1:
+                    nc.vector.tensor_copy(
+                        packed_walk(rb, c0, c1)[:, :, t - 1 : t + 1, :], planes_walk(res, c0, c1)[:, :, t - 1 : t + 1, :]
+                    )
             if c0 != last0:
                 nc.sync.dma_start(out=out_rows[:, :, c0:c1], in_=res[:, :, c0:c1])
-            nc.vector.tensor_copy(packed_walk(rb, c0, c1), planes_walk(res, c0, c1))
+                nc.vector.tensor_copy(packed_walk(rb, c0, c1), planes_walk(res, c0, c1))
             nc.vector.quantize_mx(
                 out=rw[:, c0:c1].bitcast(FP8X4), scales=rs[:, c0:c1], in_=rb[:, PACK * c0 : PACK * c1]
             )
             nc.sync.dma_start(out=out_words[:, c0:c1], in_=rw[:, c0:c1].bitcast(I32))
         for q in range(4):
-            queue = nc.sync if q == 0 else nc.scalar
+            queue = nc.sync if q < 2 else nc.scalar
             queue.dma_start(
                 out=out_2[0, 4 * q : 4 * q + 4, :].bitcast(I32),
                 in_=rs[32 * q : 32 * q + 4, :].bitcast(I32),

@@ -146,26 +146,20 @@ def tile_picked_layelaegc_none_po_kernel(
         nc.vector.tensor_scalar(yg[0][:, :half], y0_low[:, :half], gn_t[:, 0:1], None, ALU.mult)
         nc.scalar.activation(yg[0][:, half:S], y0_high[:, half:S], ACT.Copy, scale=gn_t[:, 0:1])
         for t in range(PACK):
-            if t + 1 < PACK:
+            if t == 0:
+                nc.vector.tensor_scalar(yg[1][:, :S], y_parts[1][0][0][:], gn_t[:, 1:2], None, ALU.mult)
+            elif t + 1 < PACK:
                 nc.scalar.activation(
                     yg[t + 1][:, :S], y_parts[t + 1][0][0][:], ACT.Copy, scale=gn_t[:, t + 1 : t + 2]
                 )
             for bank, c0, c1 in y_parts[t]:
                 nc.scalar.activation(sz[t][:, c0:c1], bank[:, c0:c1], ACT.Abs)
 
-        def subtract(t, c0, c1):
-            nc.vector.tensor_tensor(diff[:, t, c0:c1], yg[t][:, c0:c1], fetched[:, t, c0:c1], ALU.subtract)
-
-        last = PACK - 1
-        for t in range(last):
+        for t in range(PACK):
             nc.vector.tensor_copy(fetched[:, t, :], yg[t][:].indirect(n2_t[:]))
-            if t > 0:
-                subtract(t - 1, 0, S)
-        nc.vector.tensor_copy(fetched[:, last, :half], yg[last][:].indirect(n2_t[:, : half // 16]))
-        subtract(last - 1, 0, S)
-        subtract(last, 0, half)
+            engine = nc.vector if t == PACK - 1 else nc.gpsimd
+            engine.tensor_tensor(diff[:, t, :], yg[t][:, :S], fetched[:, t, :], ALU.subtract)
 
-        zb = held.tile([P, PACK * S], BF16, name="zb", align_bytes=64)
         zw = held.tile([P, S], U32, name="zw", align_bytes=64)
         zs = held.tile([P, S], U8, name="zs", align_bytes=64)
         h_ps = [psum.tile([P, S], F32, name="h_ps%d" % t) for t in range(PACK - 1)]
@@ -181,15 +175,15 @@ def tile_picked_layelaegc_none_po_kernel(
                     scale=neg_tau[:, t : t + 1],
                 )
 
-        def weigh(c0, c1, t0, t1):
+        def weigh(zb, c0, c1, t0, t1):
             nc.vector.tensor_tensor(
-                packed_walk(zb, c0, c1)[:, :, t0:t1, :], planes_walk(diff, c0, c1)[:, :, t0:t1, :],
+                packed_walk(zb, 0, c1 - c0)[:, :, t0:t1, :], planes_walk(diff, c0, c1)[:, :, t0:t1, :],
                 planes_walk(ea, c0, c1)[:, :, t0:t1, :], ALU.mult,
             )
 
-        def second_product(c0, c1):
+        def second_product(zb, c0, c1):
             nc.vector.quantize_mx(
-                out=zw[:, c0:c1].bitcast(FP8X4), scales=zs[:, c0:c1], in_=zb[:, PACK * c0 : PACK * c1]
+                out=zw[:, c0:c1].bitcast(FP8X4), scales=zs[:, c0:c1], in_=zb[:]
             )
             for t in range(PACK):
                 cols = slice(P * t, P * (t + 1))
@@ -201,16 +195,14 @@ def tile_picked_layelaegc_none_po_kernel(
 
         for k, (c0, c1) in enumerate(CHUNKS):
             decay(c0, c1)
-            weigh(c0, c1, 0, PACK // 2 if c0 == last0 else PACK)
-            if k == 0:
-                nc.scalar.activation(fetched[:, last, half:], yg[last][:].indirect(n2_t[:, half // 16 :]), ACT.Copy)
-                subtract(last, half, S)
-            else:
+            zb = held.tile([P, PACK * (c1 - c0)], BF16, name="zb", align_bytes=64)
+            weigh(zb, c0, c1, 0, PACK // 2 if c0 == last0 else PACK)
+            if k > 0:
                 b0, b1 = CHUNKS[k - 1]
                 nc.vector.tensor_copy(h[0][:, b0:b1], h_ps[0][:, b0:b1])
             if c0 == last0:
-                weigh(c0, c1, PACK // 2, PACK)
-            second_product(c0, c1)
+                weigh(zb, c0, c1, PACK // 2, PACK)
+            second_product(zb, c0, c1)
         nc.vector.tensor_copy(h[0][:, last0:S], h0_last[:, last0:S])
         for t in range(1, PACK):
             nc.vector.tensor_copy(h[t][:, :S], h_ps[t][:])

@@ -102,8 +102,8 @@ def tile_picked_layelaegc_none_po_kernel(
         nc.sync.dma_start(n3_t[:], n3)
         for q in range(4):
             load_scale_rows(nc.sync, w2s_in, W2_ROW, w2_scales, q)
-        nc.gpsimd.dma_start(out=gn_t[:], in_=per_row(gn))
         nc.gpsimd.dma_start(out=tau_t[:], in_=per_row(tau))
+        nc.gpsimd.dma_start(out=gn_t[:], in_=per_row(gn))
         nc.gpsimd.dma_start(out=sl_t[:], in_=per_row(sl))
         nc.gpsimd.dma_start(out=th_t[:], in_=per_row(th))
 
@@ -157,8 +157,12 @@ def tile_picked_layelaegc_none_po_kernel(
 
         for t in range(PACK):
             nc.vector.tensor_copy(fetched[:, t, :], yg[t][:].indirect(n2_t[:]))
-            engine = nc.vector if t == PACK - 1 else nc.gpsimd
-            engine.tensor_tensor(diff[:, t, :], yg[t][:, :S], fetched[:, t, :], ALU.subtract)
+            if t < PACK - 1:
+                nc.gpsimd.tensor_tensor(diff[:, t, :], yg[t][:, :S], fetched[:, t, :], ALU.subtract)
+            else:
+                nc.vector.scalar_tensor_tensor(
+                    diff[:, t, :], y_parts[t][0][0][:], gn_t[:, t : t + 1], fetched[:, t, :], ALU.mult, ALU.subtract
+                )
 
         zw = held.tile([P, S], U32, name="zw", align_bytes=64)
         zs = held.tile([P, S], U8, name="zs", align_bytes=64)
@@ -207,6 +211,8 @@ def tile_picked_layelaegc_none_po_kernel(
         for t in range(1, PACK):
             nc.vector.tensor_copy(h[t][:, :S], h_ps[t][:])
 
+        h_narrow = held.tile([P, S], F32, name="h_narrow")
+        nc.vector.tensor_copy(h_narrow[:], h_ps[PACK - 1][:])
         res = held.tile([P, PACK, S], F32, name="res")
         rb = held.tile([P, PACK * S], BF16, name="rb", align_bytes=64)
         rw = held.tile([P, S], U32, name="rw", align_bytes=64)
@@ -214,22 +220,25 @@ def tile_picked_layelaegc_none_po_kernel(
         out_rows = out_0.rearrange("(p t) c -> p t c", t=PACK)
         out_words = words(out_1)
 
-        for c0, c1 in CHUNKS:
+        def count_and_max(window, t, c0, c1):
             n = c1 - c0
+            sg = ring.tile([P, MEMBERS * n], F32, name="sg")
+            cnt = ring.tile([P, n], F32, name="cnt")
+            nc.scalar.activation(
+                sg[:], window[:].indirect(n3_t[:, MEMBERS * c0 // 16 : MEMBERS * c1 // 16]),
+                ACT.Sigmoid, bias=neg_sl_th[:, t : t + 1], scale=sl_t[:, t : t + 1],
+            )
+            nc.vector.tensor_reduce(cnt[:], sg[:].rearrange("p (j m) -> p j m", m=MEMBERS), AX.X, ALU.add)
+            nc.vector.scalar_tensor_tensor(res[:, t, c0:c1], cnt[:], -1.5, h[t][:, c0:c1], ALU.add, ALU.max)
+
+        for c0, c1 in CHUNKS:
             for t in range(PACK):
-                sg = ring.tile([P, MEMBERS * CHUNKS[0][1]], F32, name="sg")
-                cnt = ring.tile([P, CHUNKS[0][1]], F32, name="cnt")
-                nc.scalar.activation(
-                    sg[:, : MEMBERS * n],
-                    h[t][:].indirect(n3_t[:, MEMBERS * c0 // 16 : MEMBERS * c1 // 16]),
-                    ACT.Sigmoid, bias=neg_sl_th[:, t : t + 1], scale=sl_t[:, t : t + 1],
-                )
-                nc.vector.tensor_reduce(
-                    cnt[:, :n], sg[:, : MEMBERS * n].rearrange("p (j m) -> p j m", m=MEMBERS), AX.X, ALU.add
-                )
-                nc.vector.scalar_tensor_tensor(
-                    res[:, t, c0:c1], cnt[:, :n], -1.5, h[t][:, c0:c1], ALU.add, ALU.max
-                )
+                if c0 == last0 and t == PACK - 1:
+                    middle = (c0 + c1) // 2
+                    count_and_max(h_narrow, t, c0, middle)
+                    count_and_max(h_narrow, t, middle, c1)
+                else:
+                    count_and_max(h[t], t, c0, c1)
                 if c0 == last0:
                     queue = nc.scalar if t == PACK - 1 else nc.sync
                     queue.dma_start(out=out_rows[:, t, c0:c1], in_=res[:, t, c0:c1])

from contextlib import ExitStack

import concourse.mybir as mybir

F32 = mybir.dt.float32
BF16 = mybir.dt.bfloat16
I32 = mybir.dt.int32
U32 = mybir.dt.uint32
U16 = mybir.dt.uint16
U8 = mybir.dt.uint8
FP8X4 = mybir.dt.float8_e4m3fn_x4
ALU = mybir.AluOpType
ACT = mybir.ActivationFunctionType
AX = mybir.AxisListType

P = 128
PACK = 4
T = 2048
S = 512
MEMBERS = 4
CHUNKS = ((0, 256), (256, 384), (384, 512))
W1_ROW = 4
W2_ROW = 8
Y_WINDOW = 1024
H_WINDOW = 2048

FLOPS = 2 * 2 * 512 * 512 * 512


def tile_picked_layelaegc_none_po_kernel(
    tc, x_words, x_scales, w1_words, w1_scales, tau, gn, w2_words, w2_scales, sl, th,
    offs, n1, n2, n3, out_0, out_1, out_2,
):
    nc = tc.nc

    def words(ap):
        return ap[0].rearrange("p c r -> p (c r)").bitcast(I32)

    def per_row(ap):
        return ap.rearrange("(p t) o -> p (t o)", t=PACK)

    def load_scale_rows(queue, plane, first_row, scales, q):
        queue.dma_start(
            out=plane[32 * q + first_row : 32 * q + first_row + 4, :].bitcast(I32),
            in_=scales[0, 4 * q : 4 * q + 4, :].bitcast(I32),
        )

    def dealt(tile):
        return tile[:].rearrange("p (t m) -> p t m", t=PACK)

    def as_loaded(tile):
        return tile[:].rearrange("p (m t) -> p t m", t=PACK)

    def planes_walk(tile, c0, c1):
        return tile[:, :, c0:c1].rearrange("p t (c i) -> p c t i", i=4)

    def packed_walk(tile, c0, c1):
        return tile[:, PACK * c0 : PACK * c1].rearrange("p (c i t) -> p c t i", i=4, t=PACK)

    with ExitStack() as ctx:
        held = ctx.enter_context(tc.tile_pool(name="held", bufs=1))
        ring = ctx.enter_context(tc.tile_pool(name="ring", bufs=3))
        psum = ctx.enter_context(tc.psum_pool(name="psum", bufs=1))

        offs_t = held.tile([P, S // 16], U16, name="offs_t")
        n1_t = held.tile([P, S // 16], U16, name="n1_t")
        n2_t = held.tile([P, S // 16], U16, name="n2_t")
        n3_t = held.tile([P, MEMBERS * S // 16], U16, name="n3_t")
        xw = held.tile([P, T], U32, name="xw", align_bytes=64)
        xs = held.tile([P, T], U8, name="xs", align_bytes=64)
        w1w_in = held.tile([P, S], U32, name="w1w_in", align_bytes=64)
        w2w_in = held.tile([P, S], U32, name="w2w_in", align_bytes=64)
        w1s_in = held.tile([P, S], U8, name="w1s_in", align_bytes=64)
        w2s_in = held.tile([P, S], U8, name="w2s_in", align_bytes=64)
        w1w = held.tile([P, S], U32, name="w1w", align_bytes=64)
        w2w = held.tile([P, S], U32, name="w2w", align_bytes=64)
        w1s = held.tile([P, S], U8, name="w1s", align_bytes=64)
        w2s = held.tile([P, S], U8, name="w2s", align_bytes=64)
        gn_t = held.tile([P, PACK], F32, name="gn_t")
        tau_t = held.tile([P, PACK], F32, name="tau_t")
        sl_t = held.tile([P, PACK], F32, name="sl_t")
        th_t = held.tile([P, PACK], F32, name="th_t")
        neg_tau = held.tile([P, PACK], F32, name="neg_tau")
        sl_th = held.tile([P, PACK], F32, name="sl_th")
        neg_sl_th = held.tile([P, PACK], F32, name="neg_sl_th")

        nc.vector.memset(xs[:].bitcast(I32), 0)
        nc.vector.memset(w1s_in[:].bitcast(I32), 0)
        nc.gpsimd.memset(w2s_in[:].bitcast(I32), 0)

        nc.sync.dma_start(offs_t[:], offs)
        nc.sync.dma_start(out=xw[:, : T // 2].bitcast(I32), in_=words(x_words)[:, : T // 2])
        for q in range(4):
            load_scale_rows(nc.sync, xs, 0, x_scales, q)
        nc.sync.dma_start(out=xw[:, T // 2 :].bitcast(I32), in_=words(x_words)[:, T // 2 :])
        for q in range(4):
            load_scale_rows(nc.sync, w1s_in, W1_ROW, w1_scales, q)
        nc.sync.dma_start(out=w1w_in[:].bitcast(I32), in_=words(w1_words))
        nc.sync.dma_start(n2_t[:], n2)
        nc.sync.dma_start(n1_t[:], n1)
        nc.sync.dma_start(out=w2w_in[:].bitcast(I32), in_=words(w2_words))
        nc.sync.dma_start(n3_t[:], n3)
        for q in range(4):
            load_scale_rows(nc.sync, w2s_in, W2_ROW, w2_scales, q)
        nc.gpsimd.dma_start(out=tau_t[:], in_=per_row(tau))
        nc.gpsimd.dma_start(out=gn_t[:], in_=per_row(gn))
        nc.gpsimd.dma_start(out=sl_t[:], in_=per_row(sl))
        nc.gpsimd.dma_start(out=th_t[:], in_=per_row(th))

        nc.scalar.activation(neg_tau[:], tau_t[:], ACT.Copy, scale=-1.0)
        for t in range(PACK):
            nc.scalar.copy(w1w[:, P * t : P * (t + 1)], w1w_in[:, t::PACK])

        gw = held.tile([P, S], U32, name="gw", align_bytes=64)
        gs = held.tile([P, S], U8, name="gs", align_bytes=64)
        nc.vector.tensor_copy(gs[:], xs[:].indirect(offs_t[:]))
        nc.vector.tensor_copy(gw[:], xw[:].indirect(offs_t[:]))
        for t in range(PACK):
            nc.vector.tensor_copy(w1s[:, P * t : P * (t + 1)], w1s_in[:, t::PACK])

        nc.gpsimd.tensor_tensor(sl_th[:], sl_t[:], th_t[:], ALU.mult)
        nc.gpsimd.tensor_scalar(neg_sl_th[:], sl_th[:], -1.0, 0.0, ALU.mult, ALU.add)
        nc.gpsimd.tensor_copy(dealt(w2w), as_loaded(w2w_in))
        nc.gpsimd.tensor_copy(dealt(w2s), as_loaded(w2s_in))

        half = S // 2
        y0_low = psum.tile([P, S], F32, name="bank_a")
        y0_high = psum.tile([P, S], F32, name="bank_b")
        y_parts = [[(y0_low, 0, half), (y0_high, half, S)]]
        for t in range(1, PACK):
            y_parts.append([(psum.tile([P, S], F32, name="y_ps%d" % t), 0, S)])
        for t in range(PACK):
            cols = slice(P * t, P * (t + 1))
            for bank, c0, c1 in y_parts[t]:
                nc.tensor.matmul_mx(
                    out=bank[:, c0:c1], lhsT=w1w[:, cols].bitcast(FP8X4), lhsT_scale=w1s[W1_ROW:P, cols],
                    rhs=gw[:, c0:c1].bitcast(FP8X4), rhs_scale=gs[:, c0:c1], start=True, stop=True,
                )

        yg = [held.tile([P, Y_WINDOW], F32, name="yg%d" % t) for t in range(PACK)]
        sz = [held.tile([P, S], F32, name="sz%d" % t) for t in range(PACK)]
        fetched = held.tile([P, PACK, S], F32, name="fetched")
        diff = held.tile([P, PACK, S], F32, name="diff")
        ea = held.tile([P, PACK, S], F32, name="ea")

        nc.vector.tensor_scalar(yg[0][:, :half], y0_low[:, :half], gn_t[:, 0:1], None, ALU.mult)
        nc.scalar.activation(yg[0][:, half:S], y0_high[:, half:S], ACT.Copy, scale=gn_t[:, 0:1])
        for t in range(PACK):
            if t == 0:
                nc.vector.tensor_scalar(yg[1][:, :S], y_parts[1][0][0][:], gn_t[:, 1:2], None, ALU.mult)
            elif t + 1 < PACK:
                nc.scalar.activation(
                    yg[t + 1][:, :S], y_parts[t + 1][0][0][:], ACT.Copy, scale=gn_t[:, t + 1 : t + 2]
                )
            for bank, c0, c1 in y_parts[t]:
                nc.scalar.activation(sz[t][:, c0:c1], bank[:, c0:c1], ACT.Abs)

        for t in range(PACK):
            nc.vector.tensor_copy(fetched[:, t, :], yg[t][:].indirect(n2_t[:]))
            if t < PACK - 1:
                nc.gpsimd.tensor_tensor(diff[:, t, :], yg[t][:, :S], fetched[:, t, :], ALU.subtract)
            else:
                nc.vector.scalar_tensor_tensor(
                    diff[:, t, :], y_parts[t][0][0][:], gn_t[:, t : t + 1], fetched[:, t, :], ALU.mult, ALU.subtract
                )

        zw = held.tile([P, S], U32, name="zw", align_bytes=64)
        zs = held.tile([P, S], U8, name="zs", align_bytes=64)
        h_ps = [psum.tile([P, S], F32, name="h_ps%d" % t) for t in range(PACK - 1)]
        h_ps.append(psum.tile([P, S], F32, name="bank_b"))
        h = [held.tile([P, H_WINDOW], F32, name="h%d" % t) for t in range(PACK)]
        last0 = CHUNKS[-1][0]
        h0_last = psum.tile([P, S], F32, name="bank_a")

        def decay(c0, c1):
            for t in range(PACK):
                nc.scalar.activation(
                    ea[:, t, c0:c1], sz[t][:].indirect(n1_t[:, c0 // 16 : c1 // 16]), ACT.Exp,
                    scale=neg_tau[:, t : t + 1],
                )

        def weigh(zb, c0, c1, t0, t1):
            nc.vector.tensor_tensor(
                packed_walk(zb, 0, c1 - c0)[:, :, t0:t1, :], planes_walk(diff, c0, c1)[:, :, t0:t1, :],
                planes_walk(ea, c0, c1)[:, :, t0:t1, :], ALU.mult,
            )

        def second_product(zb, c0, c1):
            nc.vector.quantize_mx(
                out=zw[:, c0:c1].bitcast(FP8X4), scales=zs[:, c0:c1], in_=zb[:]
            )
            for t in range(PACK):
                cols = slice(P * t, P * (t + 1))
                bank = h0_last if (t == 0 and c0 == last0) else h_ps[t]
                nc.tensor.matmul_mx(
                    out=bank[:, c0:c1], lhsT=w2w[:, cols].bitcast(FP8X4), lhsT_scale=w2s[W2_ROW:P, cols],
                    rhs=zw[:, c0:c1].bitcast(FP8X4), rhs_scale=zs[:, c0:c1], start=True, stop=True,
                )

        for k, (c0, c1) in enumerate(CHUNKS):
            decay(c0, c1)
            zb = held.tile([P, PACK * (c1 - c0)], BF16, name="zb", align_bytes=64)
            weigh(zb, c0, c1, 0, PACK // 2 if c0 == last0 else PACK)
            if k > 0:
                b0, b1 = CHUNKS[k - 1]
                nc.vector.tensor_copy(h[0][:, b0:b1], h_ps[0][:, b0:b1])
            if c0 == last0:
                weigh(zb, c0, c1, PACK // 2, PACK)
            second_product(zb, c0, c1)
        nc.vector.tensor_copy(h[0][:, last0:S], h0_last[:, last0:S])
        for t in range(1, PACK):
            nc.vector.tensor_copy(h[t][:, :S], h_ps[t][:])

        h_narrow = held.tile([P, S], F32, name="h_narrow")
        nc.vector.tensor_copy(h_narrow[:], h_ps[PACK - 1][:])
        res = held.tile([P, PACK, S], F32, name="res")
        rb = held.tile([P, PACK * S], BF16, name="rb", align_bytes=64)
        rw = held.tile([P, S], U32, name="rw", align_bytes=64)
        rs = held.tile([P, S], U8, name="rs", align_bytes=64)
        out_rows = out_0.rearrange("(p t) c -> p t c", t=PACK)
        out_words = words(out_1)

        def count_and_max(window, t, c0, c1):
            n = c1 - c0
            sg = ring.tile([P, MEMBERS * n], F32, name="sg")
            cnt = ring.tile([P, n], F32, name="cnt")
            nc.scalar.activation(
                sg[:], window[:].indirect(n3_t[:, MEMBERS * c0 // 16 : MEMBERS * c1 // 16]),
                ACT.Sigmoid, bias=neg_sl_th[:, t : t + 1], scale=sl_t[:, t : t + 1],
            )
            nc.vector.tensor_reduce(cnt[:], sg[:].rearrange("p (j m) -> p j m", m=MEMBERS), AX.X, ALU.add)
            nc.vector.scalar_tensor_tensor(res[:, t, c0:c1], cnt[:], -1.5, h[t][:, c0:c1], ALU.add, ALU.max)

        for c0, c1 in CHUNKS:
            for t in range(PACK):
                if c0 == last0 and t == PACK - 1:
                    middle = (c0 + c1) // 2
                    count_and_max(h_narrow, t, c0, middle)
                    count_and_max(h_narrow, t, middle, c1)
                else:
                    count_and_max(h[t], t, c0, c1)
                if c0 == last0:
                    queue = nc.scalar if t == PACK - 1 else nc.sync
                    queue.dma_start(out=out_rows[:, t, c0:c1], in_=res[:, t, c0:c1])
                if c0 == last0 and t % 2 == 1:
                    nc.vector.tensor_copy(
                        packed_walk(rb, c0, c1)[:, :, t - 1 : t + 1, :], planes_walk(res, c0, c1)[:, :, t - 1 : t + 1, :]
                    )
            if c0 != last0:
                nc.sync.dma_start(out=out_rows[:, :, c0:c1], in_=res[:, :, c0:c1])
                nc.vector.tensor_copy(packed_walk(rb, c0, c1), planes_walk(res, c0, c1))
            nc.vector.quantize_mx(
                out=rw[:, c0:c1].bitcast(FP8X4), scales=rs[:, c0:c1], in_=rb[:, PACK * c0 : PACK * c1]
            )
            nc.sync.dma_start(out=out_words[:, c0:c1], in_=rw[:, c0:c1].bitcast(I32))
        for q in range(4):
            queue = nc.sync if q < 2 else nc.scalar
            queue.dma_start(
                out=out_2[0, 4 * q : 4 * q + 4, :].bitcast(I32),
                in_=rs[32 * q : 32 * q + 4, :].bitcast(I32),
            )
